import numpy as np
import ml_dtypes

BF16 = ml_dtypes.bfloat16


def bf(x):
    return np.asarray(x, np.float32).astype(BF16)


def f32(x):
    return np.asarray(x, np.float32)


def f64(x):
    return np.asarray(x).astype(np.float64)


def striped(idx):
    return np.tile(idx.reshape(-1, 16).T, (8, 1))


S, K, M, N = 512, 128, 128, 512


def setup_inputs():
    return {"base": bf(np.random.standard_normal((M, S))), "x": bf(np.random.standard_normal((K, N))), "w": bf(np.random.standard_normal((K, M)) / np.sqrt(K)), "b": f32(0.5 * np.random.standard_normal((M, 1))), "offs": striped(np.random.permutation(S))}


def reference(base, x, w, b, offs):
    idx = offs[:16].T.reshape(-1)
    z = f64(base).copy()
    z[:, idx] += f64(w).T @ f64(x)
    return z + f64(b)

@@ -1,0 +1,40 @@
+import concourse.mybir as mybir
+from concourse.masks import make_identity
+
+K = 128
+M = 128
+S = 512
+N = 512
+
+BF16, F32, U16 = mybir.dt.bfloat16, mybir.dt.float32, mybir.dt.uint16
+
+FLOPS = 2 * K * M * N
+
+
+def tile_scatter_matmul_kernel(tc, base, x, w, b, offs, out):
+    nc = tc.nc
+    with (
+        tc.tile_pool(name="sbuf", bufs=1) as sbuf,
+        tc.psum_pool(name="psum", bufs=1) as psum,
+    ):
+        base_tile = sbuf.tile([M, S], BF16, name="base_tile")
+        x_tile = sbuf.tile([K, N], BF16, name="x_tile")
+        w_tile = sbuf.tile([K, M], BF16, name="w_tile")
+        offsets = sbuf.tile([128, N // 16], U16, name="offsets")
+        bias = sbuf.tile([M, 1], F32, name="bias")
+        ident = sbuf.tile([M, M], BF16, name="ident")
+        result = sbuf.tile([M, S], F32, name="result")
+        window = psum.tile([M, S], F32, name="window")
+
+        nc.sync.dma_start(base_tile[:], base)
+        nc.sync.dma_start(x_tile[:], x)
+        nc.sync.dma_start(w_tile[:], w)
+        nc.sync.dma_start(offsets[:], offs)
+        nc.sync.dma_start(bias[:], b)
+        make_identity(nc, ident[:])
+
+        nc.tensor.matmul(window[:], ident[:], base_tile[:], start=True, stop=False)
+        nc.tensor.matmul(window[:].indirect(offsets[:]), w_tile[:], x_tile[:], start=False, stop=True)
+
+        nc.vector.tensor_scalar_add(result[:], window[:], bias[:])
+        nc.sync.dma_start(out, result[:])

@@ -5,6 +5,8 @@ K = 128
 M = 128
 S = 512
 N = 512
+WARM_COLUMNS = 256
+WARM_UPS = 6
 
 BF16, F32, U16 = mybir.dt.bfloat16, mybir.dt.float32, mybir.dt.uint16
 
@@ -25,12 +27,18 @@ def tile_scatter_matmul_kernel(tc, base, x, w, b, offs, out):
         ident = sbuf.tile([M, M], BF16, name="ident")
         result = sbuf.tile([M, S], F32, name="result")
         window = psum.tile([M, S], F32, name="window")
+        zeros = sbuf.tile([K, WARM_COLUMNS], BF16, name="zeros")
+        spare = psum.tile([M, WARM_COLUMNS], F32, name="spare")
 
         nc.sync.dma_start(base_tile[:], base)
         nc.sync.dma_start(x_tile[:], x)
         nc.sync.dma_start(w_tile[:], w)
         nc.sync.dma_start(offsets[:], offs)
         nc.sync.dma_start(bias[:], b)
+
+        nc.gpsimd.memset(zeros[:], 0.0)
+        for warm in range(WARM_UPS):
+            nc.tensor.matmul(spare[:], zeros[:, :M], zeros[:], start=True, stop=True)
         make_identity(nc, ident[:])
 
         nc.tensor.matmul(window[:], ident[:], base_tile[:], start=True, stop=False)

import concourse.mybir as mybir
from concourse.masks import make_identity

K = 128
M = 128
S = 512
N = 512
WARM_COLUMNS = 256
WARM_UPS = 6

BF16, F32, U16 = mybir.dt.bfloat16, mybir.dt.float32, mybir.dt.uint16

FLOPS = 2 * K * M * N


def tile_scatter_matmul_kernel(tc, base, x, w, b, offs, out):
    nc = tc.nc
    with (
        tc.tile_pool(name="sbuf", bufs=1) as sbuf,
        tc.psum_pool(name="psum", bufs=1) as psum,
    ):
        base_tile = sbuf.tile([M, S], BF16, name="base_tile")
        x_tile = sbuf.tile([K, N], BF16, name="x_tile")
        w_tile = sbuf.tile([K, M], BF16, name="w_tile")
        offsets = sbuf.tile([128, N // 16], U16, name="offsets")
        bias = sbuf.tile([M, 1], F32, name="bias")
        ident = sbuf.tile([M, M], BF16, name="ident")
        result = sbuf.tile([M, S], F32, name="result")
        window = psum.tile([M, S], F32, name="window")
        zeros = sbuf.tile([K, WARM_COLUMNS], BF16, name="zeros")
        spare = psum.tile([M, WARM_COLUMNS], F32, name="spare")

        nc.sync.dma_start(base_tile[:], base)
        nc.sync.dma_start(x_tile[:], x)
        nc.sync.dma_start(w_tile[:], w)
        nc.sync.dma_start(offsets[:], offs)
        nc.sync.dma_start(bias[:], b)

        nc.gpsimd.memset(zeros[:], 0.0)
        for warm in range(WARM_UPS):
            nc.tensor.matmul(spare[:], zeros[:, :M], zeros[:], start=True, stop=True)
        make_identity(nc, ident[:])

        nc.tensor.matmul(window[:], ident[:], base_tile[:], start=True, stop=False)
        nc.tensor.matmul(window[:].indirect(offsets[:]), w_tile[:], x_tile[:], start=False, stop=True)

        nc.vector.tensor_scalar_add(result[:], window[:], bias[:])
        nc.sync.dma_start(out, result[:])
